import numpy as np
import ml_dtypes


def mxq(x, axis, fmt="e4m3"):
    dtype, down = {"e4m3": (ml_dtypes.float8_e4m3fn, 7), "e5m2": (ml_dtypes.float8_e5m2, 14)}[fmt]
    v = np.moveaxis(np.asarray(x, np.float32).astype(ml_dtypes.bfloat16).astype(np.float64), axis, -1)
    blocks = v.reshape(v.shape[:-1] + (-1, 32))
    amax = np.abs(blocks).max(-1, keepdims=True)
    byte = np.maximum(np.where(amax > 0, np.frexp(amax)[1] - 1 + 127, 0) - down, 1)
    scale = np.exp2(byte - 127.0)
    codes = (blocks / scale).astype(np.float32).astype(dtype).astype(np.float64)
    return np.moveaxis((codes * scale).reshape(v.shape), -1, axis)


WIDE = False


def mx_kscale(k):
    if not WIDE:
        return np.ones(k)
    levels = np.array([10, -10, 5, -5, 0])
    if k % 512:
        return np.exp2(np.random.permutation(np.resize(levels, k // 32))).repeat(32)
    a = np.empty((k // 512, 16))
    for p in range(k // 512):
        a[p, :8] = np.random.permutation(np.resize(levels, 8))
        for g in range(8):
            far = levels[np.abs(levels - a[p, g]) >= 10]
            a[p, g + 8] = far[np.random.randint(len(far))]
    return np.exp2(a.ravel()).repeat(32)


def f64(x):
    return np.asarray(x).astype(np.float64)


def striped(idx):
    return np.tile(idx.reshape(-1, 16).T, (8, 1)).astype(np.uint16)


def unstriped(offs):
    return offs[:16].T.reshape(-1).astype(np.int64)


def striped8(idx):
    return np.concatenate([x.reshape(-1, 16).T for x in idx]).astype(np.uint16)


def runs(offs, k):
    lists = np.stack([offs[16 * r : 16 * r + 16].T.reshape(-1) for r in range(8)]).astype(np.int64)
    return lists[np.arange(k) % 512 // 64]


def pack_weight(w):
    k, n = w.shape
    w = f64(np.asarray(w, np.float32).astype(ml_dtypes.bfloat16)).reshape(k // 32, 32, n)
    amax = np.abs(w).max(1)
    byte = np.clip(np.where(amax > 0, np.frexp(amax)[1] - 1 + 127 - 7, 1), 1, 254)
    scaled = (w * np.exp2(127.0 - byte)[:, None, :]).reshape(k, n).astype(np.float32)
    words = np.ascontiguousarray(scaled.reshape(k // 512, 128, 4, n).transpose(0, 1, 3, 2)).astype(ml_dtypes.float8_e4m3fn).view(np.uint8)
    return words, np.ascontiguousarray(byte.astype(np.uint8).reshape(k // 512, 16, n))


def unpack_weight(words, scales):
    g, p, n, _ = words.shape
    vals = np.ascontiguousarray(words).view(ml_dtypes.float8_e4m3fn).astype(np.float64) * np.repeat(np.exp2(scales.astype(np.float64) - 127.0), 8, axis=1)[..., None]
    return vals.transpose(0, 1, 3, 2).reshape(g * 512, n)


K, T, S, N, G, H = 512, 2048, 512, 512, 2048, 512


def setup_inputs():
    n = np.random.standard_normal
    s = mx_kscale(K)[:, None]
    u = mx_kscale(S)
    packed_xT = pack_weight(n((K, T)) * s)
    packed_dT = pack_weight(n((K, G)) / s)
    return {
        "x_words": packed_xT[0],
        "x_scales": packed_xT[1],
        "d_words": packed_dT[0],
        "d_scales": packed_dT[1],
        "gn": (np.random.uniform(0.5, 1.5, (H, 1)) * u[:, None]).astype(np.float32),
        "w1": (n((H, N)) / np.sqrt(H) / u[:, None]).astype(np.float32),
        "offs": striped(np.random.permutation(T)[:S]),
        "k1": striped8(np.random.randint(0, G, (8, H))),
        "n1": striped(np.random.permutation(S)),
        "n2": striped8(np.stack([np.random.permutation(S) for _ in range(8)])),
        "n3": striped8(np.stack([np.random.permutation(S) for _ in range(8)])),
    }


def reference(x_words, x_scales, d_words, d_scales, gn, w1, offs, k1, n1, n2, n3):
    d_k1 = unpack_weight(d_words, d_scales)[np.arange(K)[:, None], runs(k1, K)]
    xq = unpack_weight(x_words, x_scales)[:, unstriped(offs)]
    h = 0.0625 * (d_k1.T @ xq)
    pa = h[:, unstriped(n1)]
    z = f64(gn) * ((2.0 * (h * pa)) / ((h) ** 2 + (pa) ** 2 + 0.5))
    h2 = mxq(f64(w1), 0, "e4m3").T @ mxq(z, 0, "e4m3")
    return (h2[np.arange(N)[:, None], runs(n2, N)]) * (h2[np.arange(N)[:, None], runs(n3, N)])

@@ -1,0 +1,181 @@
+from contextlib import ExitStack
+
+import concourse.mybir as mybir
+
+K, T, S, N, G, H = 512, 2048, 512, 512, 2048, 512
+FLOPS = 2 * K * H * S + 2 * H * N * S
+
+F32 = mybir.dt.float32
+BF16 = mybir.dt.bfloat16
+I32 = mybir.dt.int32
+U32 = mybir.dt.uint32
+U16 = mybir.dt.uint16
+U8 = mybir.dt.uint8
+FP8X4 = mybir.dt.float8_e4m3fn_x4
+ACT = mybir.ActivationFunctionType
+ALU = mybir.AluOpType
+
+P = 128
+PACK = 4
+PER_COL = 16
+CHUNK = 128
+HALF = 256
+
+
+def entries(lst, first, count):
+    return lst[:, first // PER_COL : (first + count) // PER_COL]
+
+
+def tile_picked_pqlayharmprod_none_p_kernel(
+    tc, x_words, x_scales, d_words, d_scales, gn, w1, offs, k1, n1, n2, n3, out
+):
+    nc = tc.nc
+    with ExitStack() as ctx:
+        keep = ctx.enter_context(tc.tile_pool(name="keep", bufs=1))
+        psum = ctx.enter_context(tc.psum_pool(name="psum", bufs=1))
+
+        def list_tile(name, dram):
+            lst = keep.tile([P, S // PER_COL], U16, name=name)
+            nc.sync.dma_start(lst[:], dram)
+            return lst
+
+        d_sc_table = keep.tile([P, G], U8, name="d_sc_table")
+        x_sc_table = keep.tile([P, T], U8, name="x_sc_table")
+        nc.vector.memset(d_sc_table[:].bitcast(I32), 0)
+        nc.vector.memset(x_sc_table[:].bitcast(I32), 0)
+        k1_list = list_tile("k1_list", k1)
+        offs_list = list_tile("offs_list", offs)
+        n1_list = list_tile("n1_list", n1)
+        n2_list = list_tile("n2_list", n2)
+        n3_list = list_tile("n3_list", n3)
+        d_rows = d_scales[0].bitcast(I32).rearrange("(r e) c -> e r c", e=2)
+        for e in range(2):
+            nc.sync.dma_start(d_sc_table[e:P:16, :].bitcast(I32), d_rows[e])
+        d_table = keep.tile([P, G], I32, name="d_table")
+        nc.sync.dma_start(d_table[:], d_words[0].rearrange("p n t -> p (n t)").bitcast(I32))
+        x_rows = x_scales[0].bitcast(I32)
+        for q in range(4):
+            nc.sync.dma_start(x_sc_table[32 * q : 32 * q + 4, :].bitcast(I32), x_rows[4 * q : 4 * q + 4, :])
+        x_table = keep.tile([P, T], I32, name="x_table")
+        nc.sync.dma_start(x_table[:], x_words[0].rearrange("p n t -> p (n t)").bitcast(I32))
+        w_raw = []
+        for half in range(2):
+            raw = keep.tile([P, PACK, HALF], F32, name="w_raw%d" % half)
+            nc.sync.dma_start(raw[:], w1.rearrange("(p j) m -> p j m", j=PACK)[:, :, half * HALF : (half + 1) * HALF])
+            w_raw.append(raw)
+        gain = keep.tile([P, PACK], F32, name="gain")
+        nc.sync.dma_start(gain[:], gn.rearrange("(p t) o -> p (t o)", t=PACK))
+
+        d_sc_got = keep.tile([P, H], U8, name="d_sc_got")
+        nc.vector.tensor_copy(d_sc_got[:], d_sc_table[:].indirect(k1_list[:]))
+        d_sc = keep.tile([P, H], U8, name="d_sc", align_bytes=64)
+        nc.vector.tensor_copy(
+            d_sc[:].rearrange("p (t a i) -> p a t i", t=PACK, i=4),
+            d_sc_got[:].rearrange("p (a i t) -> p a t i", t=PACK, i=4),
+        )
+        for e in range(2):
+            nc.scalar.dma_start(d_sc[2 + e : P : 32, :].bitcast(I32), d_sc[16 + e : P : 32, :].bitcast(I32))
+
+        d_got = keep.tile([P, H], U32, name="d_got")
+        nc.vector.tensor_copy(d_got[:], d_table[:].bitcast(U32).indirect(k1_list[:]))
+        d_codes = keep.tile([P, H], U32, name="d_codes", align_bytes=64)
+        nc.vector.tensor_copy(
+            d_codes[:].rearrange("p (t a i) -> p a t i", t=PACK, i=4),
+            d_got[:].rearrange("p (a i t) -> p a t i", t=PACK, i=4),
+        )
+        x_sc = keep.tile([P, S], U8, name="x_sc", align_bytes=64)
+        nc.vector.tensor_copy(x_sc[:], x_sc_table[:].indirect(offs_list[:]))
+        x_codes = keep.tile([P, S], U32, name="x_codes", align_bytes=64)
+        for half in range(2):
+            js = slice(half * HALF, (half + 1) * HALF)
+            nc.vector.tensor_copy(x_codes[:, js], x_table[:].bitcast(U32).indirect(entries(offs_list, half * HALF, HALF)))
+
+        h = [keep.tile([P, S], F32, name="h%d" % t) for t in range(PACK)]
+        h_sq = keep.tile([P, PACK, S], F32, name="h_sq")
+        acc = [psum.tile([P, S], F32, name="h_acc%d" % t) for t in range(PACK)]
+        for half in range(2):
+            js = slice(half * HALF, (half + 1) * HALF)
+            for t in range(PACK):
+                cols = slice(t * P, (t + 1) * P)
+                nc.tensor.matmul_mx(
+                    out=acc[t][:, js], lhsT=d_codes[:, cols].bitcast(FP8X4), lhsT_scale=d_sc[:, cols],
+                    rhs=x_codes[:, js].bitcast(FP8X4), rhs_scale=x_sc[:, js], start=True, stop=True,
+                )
+        for t in range(PACK):
+            if t % 2 == 0:
+                nc.scalar.activation(h[t][:], acc[t][:], ACT.Copy, scale=0.0625)
+            else:
+                nc.vector.tensor_scalar_mul(h[t][:], acc[t][:], 0.0625)
+        w_bf = keep.tile([P, PACK * N], BF16, name="w_bf", align_bytes=64)
+        w_view = w_bf[:].rearrange("p (t u e j) -> p u t j e", t=PACK, e=4, j=PACK)
+        for half, copy in enumerate((nc.scalar.copy, nc.vector.tensor_copy)):
+            copy(
+                w_view[:, 16 * half : 16 * (half + 1)],
+                w_raw[half][:].rearrange("p j (u t e) -> p u t j e", t=PACK, e=4),
+            )
+        for t in range(PACK):
+            nc.scalar.activation(h_sq[:, t, :], acc[t][:], ACT.Square, scale=0.0625)
+
+        nums, invs = [], []
+        for c in range(2):
+            js = slice(c * HALF, (c + 1) * HALF)
+            pa = keep.tile([P, PACK, HALF], F32, name="pa%d" % c)
+            for t in range(PACK):
+                looked_up = h[t][:].indirect(entries(n1_list, c * HALF, HALF))
+                if t < PACK - 1:
+                    nc.vector.tensor_copy(pa[:, t, :], looked_up)
+                else:
+                    nc.scalar.activation(pa[:, t, :], looked_up, ACT.Copy)
+            pa_sq = keep.tile([P, PACK, HALF], F32, name="pa_sq%d" % c, tag="sq_num%d" % c)
+            nc.scalar.activation(pa_sq[:], pa[:], ACT.Square)
+            both = keep.tile([P, PACK, HALF], F32, name="both%d" % c)
+            nc.vector.tensor_tensor(both[:], pa_sq[:], h_sq[:, :, js], ALU.add)
+            root = keep.tile([P, PACK, HALF], F32, name="root%d" % c)
+            nc.scalar.activation(root[:], both[:], ACT.Abs_reciprocal_sqrt, bias=0.25, scale=0.5)
+            inv = keep.tile([P, PACK, HALF], F32, name="inv%d" % c)
+            nc.scalar.activation(inv[:], root[:], ACT.Square)
+            num = keep.tile([P, PACK, HALF], F32, name="num%d" % c, tag="sq_num%d" % c)
+            for t in range(PACK):
+                nc.vector.scalar_tensor_tensor(num[:, t, :], h[t][:, js], gain[:, t : t + 1], pa[:, t, :], ALU.mult, ALU.mult)
+            nums.append(num)
+            invs.append(inv)
+
+        w_codes = keep.tile([P, N], U32, name="w_codes", align_bytes=64)
+        w_sc = keep.tile([P, N], U8, name="w_sc", align_bytes=64)
+        nc.vector.quantize_mx(out=w_codes[:].bitcast(FP8X4), scales=w_sc[:], in_=w_bf[:])
+
+        h2 = [keep.tile([P, S], F32, name="h2_%d" % t) for t in range(PACK)]
+        acc2 = [psum.tile([P, S], F32, name="h2_acc%d" % t) for t in range(PACK)]
+        for c in range(2):
+            js = slice(c * HALF, (c + 1) * HALF)
+            z_bf = keep.tile([P, HALF * PACK], BF16, name="z_bf%d" % c, align_bytes=64)
+            nc.vector.tensor_tensor(
+                z_bf[:].rearrange("p (a i t) -> p a t i", t=PACK, i=4),
+                nums[c][:].rearrange("p t (a i) -> p a t i", i=4),
+                invs[c][:].rearrange("p t (a i) -> p a t i", i=4),
+                ALU.mult,
+            )
+            z_codes = keep.tile([P, HALF], U32, name="z_codes%d" % c, align_bytes=64)
+            z_sc = keep.tile([P, HALF], U8, name="z_sc%d" % c, align_bytes=64)
+            nc.vector.quantize_mx(out=z_codes[:].bitcast(FP8X4), scales=z_sc[:], in_=z_bf[:])
+            for t in range(PACK):
+                cols = slice(t * P, (t + 1) * P)
+                nc.tensor.matmul_mx(
+                    out=acc2[t][:, js], lhsT=w_codes[:, cols].bitcast(FP8X4), lhsT_scale=w_sc[:, cols],
+                    rhs=z_codes[:].bitcast(FP8X4), rhs_scale=z_sc[:], start=True, stop=True,
+                )
+                nc.scalar.copy(h2[t][:, js], acc2[t][:, js])
+
+        out_rows = out.rearrange("(u t e) j -> t u e j", t=PACK, e=4)
+        for t in range(PACK):
+            res = keep.tile([P, S], F32, name="res%d" % t)
+            for half in range(2):
+                js = slice(half * HALF, (half + 1) * HALF)
+                left = keep.tile([P, HALF], F32, name="left%d_%d" % (t, half))
+                looked_up = h2[t][:].indirect(entries(n2_list, half * HALF, HALF))
+                if t == 0 and half == 0:
+                    nc.vector.tensor_copy(left[:], looked_up)
+                else:
+                    nc.scalar.activation(left[:], looked_up, ACT.Copy)
+                nc.vector.tensor_tensor(res[:, js], h2[t][:].indirect(entries(n3_list, half * HALF, HALF)), left[:], ALU.mult)
+            nc.sync.dma_start(out_rows[t], res[:])

@@ -39,6 +39,11 @@ def tile_picked_pqlayharmprod_none_p_kernel(
             nc.sync.dma_start(lst[:], dram)
             return lst
 
+        one = keep.tile([P, 1], F32, name="one")
+        nc.gpsimd.memset(one[:], 1.0)
+        warm = keep.tile([P, 1], F32, name="warm")
+        nc.scalar.activation(warm[:], one[:], ACT.Abs_reciprocal_sqrt, bias=0.25, scale=0.5)
+
         d_sc_table = keep.tile([P, G], U8, name="d_sc_table")
         x_sc_table = keep.tile([P, T], U8, name="x_sc_table")
         nc.vector.memset(d_sc_table[:].bitcast(I32), 0)
@@ -70,8 +75,8 @@ def tile_picked_pqlayharmprod_none_p_kernel(
         nc.vector.tensor_copy(d_sc_got[:], d_sc_table[:].indirect(k1_list[:]))
         d_sc = keep.tile([P, H], U8, name="d_sc", align_bytes=64)
         nc.vector.tensor_copy(
-            d_sc[:].rearrange("p (t a i) -> p a t i", t=PACK, i=4),
-            d_sc_got[:].rearrange("p (a i t) -> p a t i", t=PACK, i=4),
+            d_sc[:].rearrange("p (t m) -> p t m", t=PACK),
+            d_sc_got[:].rearrange("p (m t) -> p t m", t=PACK),
         )
         for e in range(2):
             nc.scalar.dma_start(d_sc[2 + e : P : 32, :].bitcast(I32), d_sc[16 + e : P : 32, :].bitcast(I32))
@@ -92,33 +97,36 @@ def tile_picked_pqlayharmprod_none_p_kernel(
 
         h = [keep.tile([P, S], F32, name="h%d" % t) for t in range(PACK)]
         h_sq = keep.tile([P, PACK, S], F32, name="h_sq")
-        acc = [psum.tile([P, S], F32, name="h_acc%d" % t) for t in range(PACK)]
+        acc = {}
         for half in range(2):
             js = slice(half * HALF, (half + 1) * HALF)
             for t in range(PACK):
                 cols = slice(t * P, (t + 1) * P)
+                acc[half, t] = psum.tile([P, HALF], F32, name="h_acc%d_%d" % (half, t), tag="bank%d_%d" % (half, t))
                 nc.tensor.matmul_mx(
-                    out=acc[t][:, js], lhsT=d_codes[:, cols].bitcast(FP8X4), lhsT_scale=d_sc[:, cols],
+                    out=acc[half, t][:], lhsT=d_codes[:, cols].bitcast(FP8X4), lhsT_scale=d_sc[:, cols],
                     rhs=x_codes[:, js].bitcast(FP8X4), rhs_scale=x_sc[:, js], start=True, stop=True,
                 )
-        for t in range(PACK):
-            if t % 2 == 0:
-                nc.scalar.activation(h[t][:], acc[t][:], ACT.Copy, scale=0.0625)
-            else:
-                nc.vector.tensor_scalar_mul(h[t][:], acc[t][:], 0.0625)
+        for half in range(2):
+            js = slice(half * HALF, (half + 1) * HALF)
+            for t in range(PACK):
+                if half == 1 and t < 2:
+                    nc.vector.tensor_scalar_mul(h[t][:, js], acc[half, t][:], 0.0625)
+                else:
+                    nc.scalar.activation(h[t][:, js], acc[half, t][:], ACT.Copy, scale=0.0625)
         w_bf = keep.tile([P, PACK * N], BF16, name="w_bf", align_bytes=64)
-        w_view = w_bf[:].rearrange("p (t u e j) -> p u t j e", t=PACK, e=4, j=PACK)
-        for half, copy in enumerate((nc.scalar.copy, nc.vector.tensor_copy)):
-            copy(
-                w_view[:, 16 * half : 16 * (half + 1)],
-                w_raw[half][:].rearrange("p j (u t e) -> p u t j e", t=PACK, e=4),
+        w_view = w_bf[:].rearrange("p (t u e j) -> p u t j e", t=PACK, e=2, j=PACK)
+        for half in range(2):
+            nc.vector.tensor_copy(
+                w_view[:, 32 * half : 32 * (half + 1)],
+                w_raw[half][:].rearrange("p j (u t e) -> p u t j e", t=PACK, e=2),
             )
-        for t in range(PACK):
-            nc.scalar.activation(h_sq[:, t, :], acc[t][:], ACT.Square, scale=0.0625)
 
         nums, invs = [], []
         for c in range(2):
             js = slice(c * HALF, (c + 1) * HALF)
+            for t in range(PACK):
+                nc.scalar.activation(h_sq[:, t, js], acc[c, t][:], ACT.Square, scale=0.0625)
             pa = keep.tile([P, PACK, HALF], F32, name="pa%d" % c)
             for t in range(PACK):
                 looked_up = h[t][:].indirect(entries(n1_list, c * HALF, HALF))
@@ -145,14 +153,14 @@ def tile_picked_pqlayharmprod_none_p_kernel(
         nc.vector.quantize_mx(out=w_codes[:].bitcast(FP8X4), scales=w_sc[:], in_=w_bf[:])
 
         h2 = [keep.tile([P, S], F32, name="h2_%d" % t) for t in range(PACK)]
-        acc2 = [psum.tile([P, S], F32, name="h2_acc%d" % t) for t in range(PACK)]
+        acc2 = [psum.tile([P, S], F32, name="h2_acc%d" % t, tag="bank0_%d" % t) for t in range(PACK)]
         for c in range(2):
             js = slice(c * HALF, (c + 1) * HALF)
             z_bf = keep.tile([P, HALF * PACK], BF16, name="z_bf%d" % c, align_bytes=64)
             nc.vector.tensor_tensor(
-                z_bf[:].rearrange("p (a i t) -> p a t i", t=PACK, i=4),
-                nums[c][:].rearrange("p t (a i) -> p a t i", i=4),
-                invs[c][:].rearrange("p t (a i) -> p a t i", i=4),
+                z_bf[:].rearrange("p (a i t) -> p a t i", t=PACK, i=2),
+                nums[c][:].rearrange("p t (a i) -> p a t i", i=2),
+                invs[c][:].rearrange("p t (a i) -> p a t i", i=2),
                 ALU.mult,
             )
             z_codes = keep.tile([P, HALF], U32, name="z_codes%d" % c, align_bytes=64)
@@ -164,9 +172,12 @@ def tile_picked_pqlayharmprod_none_p_kernel(
                     out=acc2[t][:, js], lhsT=w_codes[:, cols].bitcast(FP8X4), lhsT_scale=w_sc[:, cols],
                     rhs=z_codes[:].bitcast(FP8X4), rhs_scale=z_sc[:], start=True, stop=True,
                 )
-                nc.scalar.copy(h2[t][:, js], acc2[t][:, js])
+                if c == 1 and t % 2 == 1:
+                    nc.vector.tensor_copy(h2[t][:, js], acc2[t][:, js])
+                else:
+                    nc.scalar.copy(h2[t][:, js], acc2[t][:, js])
 
-        out_rows = out.rearrange("(u t e) j -> t u e j", t=PACK, e=4)
+        out_rows = out.rearrange("(u t e) j -> t u e j", t=PACK, e=2)
         for t in range(PACK):
             res = keep.tile([P, S], F32, name="res%d" % t)
             for half in range(2):
@@ -177,5 +188,13 @@ def tile_picked_pqlayharmprod_none_p_kernel(
                     nc.vector.tensor_copy(left[:], looked_up)
                 else:
                     nc.scalar.activation(left[:], looked_up, ACT.Copy)
-                nc.vector.tensor_tensor(res[:, js], h2[t][:].indirect(entries(n3_list, half * HALF, HALF)), left[:], ALU.mult)
-            nc.sync.dma_start(out_rows[t], res[:])
+                looked_up = h2[t][:].indirect(entries(n3_list, half * HALF, HALF))
+                if t < PACK - 1:
+                    nc.vector.tensor_tensor(res[:, js], looked_up, left[:], ALU.mult)
+                else:
+                    right = keep.tile([P, HALF], F32, name="right%d" % half)
+                    nc.scalar.activation(right[:], looked_up, ACT.Copy)
+                    nc.vector.tensor_tensor(res[:, js], right[:], left[:], ALU.mult)
+                    nc.sync.dma_start(out_rows[t][:, :, js], res[:, js])
+            if t < PACK - 1:
+                nc.sync.dma_start(out_rows[t], res[:])

@@ -45,7 +45,7 @@ def tile_picked_pqlayharmprod_none_p_kernel(
         nc.scalar.activation(warm[:], one[:], ACT.Abs_reciprocal_sqrt, bias=0.25, scale=0.5)
 
         d_sc_table = keep.tile([P, G], U8, name="d_sc_table")
-        x_sc_table = keep.tile([P, T], U8, name="x_sc_table")
+        x_sc_table = keep.tile([P, T], U8, name="x_sc_table", tag="x_sc_table")
         nc.vector.memset(d_sc_table[:].bitcast(I32), 0)
         nc.vector.memset(x_sc_table[:].bitcast(I32), 0)
         k1_list = list_tile("k1_list", k1)
@@ -56,37 +56,30 @@ def tile_picked_pqlayharmprod_none_p_kernel(
         d_rows = d_scales[0].bitcast(I32).rearrange("(r e) c -> e r c", e=2)
         for e in range(2):
             nc.sync.dma_start(d_sc_table[e:P:16, :].bitcast(I32), d_rows[e])
-        d_table = keep.tile([P, G], I32, name="d_table")
+        d_table = keep.tile([P, G], I32, name="d_table", tag="d_table")
         nc.sync.dma_start(d_table[:], d_words[0].rearrange("p n t -> p (n t)").bitcast(I32))
         x_rows = x_scales[0].bitcast(I32)
         for q in range(4):
             nc.sync.dma_start(x_sc_table[32 * q : 32 * q + 4, :].bitcast(I32), x_rows[4 * q : 4 * q + 4, :])
         x_table = keep.tile([P, T], I32, name="x_table")
         nc.sync.dma_start(x_table[:], x_words[0].rearrange("p n t -> p (n t)").bitcast(I32))
-        w_raw = []
-        for half in range(2):
-            raw = keep.tile([P, PACK, HALF], F32, name="w_raw%d" % half)
-            nc.sync.dma_start(raw[:], w1.rearrange("(p j) m -> p j m", j=PACK)[:, :, half * HALF : (half + 1) * HALF])
-            w_raw.append(raw)
-        gain = keep.tile([P, PACK], F32, name="gain")
-        nc.sync.dma_start(gain[:], gn.rearrange("(p t) o -> p (t o)", t=PACK))
 
         d_sc_got = keep.tile([P, H], U8, name="d_sc_got")
         nc.vector.tensor_copy(d_sc_got[:], d_sc_table[:].indirect(k1_list[:]))
         d_sc = keep.tile([P, H], U8, name="d_sc", align_bytes=64)
         nc.vector.tensor_copy(
-            d_sc[:].rearrange("p (t m) -> p t m", t=PACK),
-            d_sc_got[:].rearrange("p (m t) -> p t m", t=PACK),
+            d_sc[:].bitcast(I32).rearrange("p (t u) -> p t u", t=PACK),
+            d_sc_got[:].bitcast(I32).rearrange("p (u t) -> p t u", t=PACK),
         )
         for e in range(2):
             nc.scalar.dma_start(d_sc[2 + e : P : 32, :].bitcast(I32), d_sc[16 + e : P : 32, :].bitcast(I32))
 
-        d_got = keep.tile([P, H], U32, name="d_got")
+        d_got = keep.tile([P, H], U32, name="d_got", tag="d_got")
         nc.vector.tensor_copy(d_got[:], d_table[:].bitcast(U32).indirect(k1_list[:]))
         d_codes = keep.tile([P, H], U32, name="d_codes", align_bytes=64)
         nc.vector.tensor_copy(
-            d_codes[:].rearrange("p (t a i) -> p a t i", t=PACK, i=4),
-            d_got[:].rearrange("p (a i t) -> p a t i", t=PACK, i=4),
+            d_codes[:].rearrange("p (t u e) -> p t u e", t=PACK, e=4),
+            d_got[:].rearrange("p (u t e) -> p t u e", t=PACK, e=4),
         )
         x_sc = keep.tile([P, S], U8, name="x_sc", align_bytes=64)
         nc.vector.tensor_copy(x_sc[:], x_sc_table[:].indirect(offs_list[:]))
@@ -95,8 +88,18 @@ def tile_picked_pqlayharmprod_none_p_kernel(
             js = slice(half * HALF, (half + 1) * HALF)
             nc.vector.tensor_copy(x_codes[:, js], x_table[:].bitcast(U32).indirect(entries(offs_list, half * HALF, HALF)))
 
+        w_raw = []
+        w_rows = w1.rearrange("(u t e) m -> t u e m", t=PACK, e=4)
+        for half in range(2):
+            raw = keep.tile([P, PACK, HALF], F32, name="w_raw%d" % half, tag=("d_table", "x_sc_table")[half])
+            for t in range(PACK):
+                nc.sync.dma_start(raw[:, t, :], w_rows[t][:, :, half * HALF : (half + 1) * HALF])
+            w_raw.append(raw)
+        gain = keep.tile([P, PACK, 8], F32, name="gain", tag="d_got")
+        for t in range(PACK):
+            nc.sync.dma_start(gain[:, t, 0:1], gn.rearrange("(u t e) o -> t u e o", t=PACK, e=4)[t])
+
         h = [keep.tile([P, S], F32, name="h%d" % t) for t in range(PACK)]
-        h_sq = keep.tile([P, PACK, S], F32, name="h_sq")
         acc = {}
         for half in range(2):
             js = slice(half * HALF, (half + 1) * HALF)
@@ -125,8 +128,9 @@ def tile_picked_pqlayharmprod_none_p_kernel(
         nums, invs = [], []
         for c in range(2):
             js = slice(c * HALF, (c + 1) * HALF)
+            h_sq = keep.tile([P, PACK, HALF], F32, name="h_sq%d" % c, tag="h_sq%d" % c, align_bytes=64)
             for t in range(PACK):
-                nc.scalar.activation(h_sq[:, t, js], acc[c, t][:], ACT.Square, scale=0.0625)
+                nc.scalar.activation(h_sq[:, t, :], acc[c, t][:], ACT.Square, scale=0.0625)
             pa = keep.tile([P, PACK, HALF], F32, name="pa%d" % c)
             for t in range(PACK):
                 looked_up = h[t][:].indirect(entries(n1_list, c * HALF, HALF))
@@ -137,18 +141,18 @@ def tile_picked_pqlayharmprod_none_p_kernel(
             pa_sq = keep.tile([P, PACK, HALF], F32, name="pa_sq%d" % c, tag="sq_num%d" % c)
             nc.scalar.activation(pa_sq[:], pa[:], ACT.Square)
             both = keep.tile([P, PACK, HALF], F32, name="both%d" % c)
-            nc.vector.tensor_tensor(both[:], pa_sq[:], h_sq[:, :, js], ALU.add)
+            nc.vector.tensor_tensor(both[:], pa_sq[:], h_sq[:], ALU.add)
             root = keep.tile([P, PACK, HALF], F32, name="root%d" % c)
             nc.scalar.activation(root[:], both[:], ACT.Abs_reciprocal_sqrt, bias=0.25, scale=0.5)
             inv = keep.tile([P, PACK, HALF], F32, name="inv%d" % c)
             nc.scalar.activation(inv[:], root[:], ACT.Square)
             num = keep.tile([P, PACK, HALF], F32, name="num%d" % c, tag="sq_num%d" % c)
             for t in range(PACK):
-                nc.vector.scalar_tensor_tensor(num[:, t, :], h[t][:, js], gain[:, t : t + 1], pa[:, t, :], ALU.mult, ALU.mult)
+                nc.vector.scalar_tensor_tensor(num[:, t, :], h[t][:, js], gain[:, t, 0:1], pa[:, t, :], ALU.mult, ALU.mult)
             nums.append(num)
             invs.append(inv)
 
-        w_codes = keep.tile([P, N], U32, name="w_codes", align_bytes=64)
+        w_codes = keep.tile([P, N], U32, name="w_codes", tag="h_sq0", align_bytes=64)
         w_sc = keep.tile([P, N], U8, name="w_sc", align_bytes=64)
         nc.vector.quantize_mx(out=w_codes[:].bitcast(FP8X4), scales=w_sc[:], in_=w_bf[:])
 
@@ -189,12 +193,13 @@ def tile_picked_pqlayharmprod_none_p_kernel(
                 else:
                     nc.scalar.activation(left[:], looked_up, ACT.Copy)
                 looked_up = h2[t][:].indirect(entries(n3_list, half * HALF, HALF))
-                if t < PACK - 1:
+                if t < PACK - 1 or half == 0:
                     nc.vector.tensor_tensor(res[:, js], looked_up, left[:], ALU.mult)
                 else:
                     right = keep.tile([P, HALF], F32, name="right%d" % half)
                     nc.scalar.activation(right[:], looked_up, ACT.Copy)
                     nc.vector.tensor_tensor(res[:, js], right[:], left[:], ALU.mult)
+                if t == PACK - 1:
                     nc.sync.dma_start(out_rows[t][:, :, js], res[:, js])
             if t < PACK - 1:
                 nc.sync.dma_start(out_rows[t], res[:])

@@ -16,14 +16,18 @@ ACT = mybir.ActivationFunctionType
 ALU = mybir.AluOpType
 
 P = 128
-PACK = 4
-PER_COL = 16
-CHUNK = 128
+TILES = 4
+GROUP = 16
+QUAD = 32
 HALF = 256
+H_SCALE = 0.0625
+
+STRETCHES = ((0, 256), (256, 128), (384, 128))
+LAST_TILE_PIECES = ((0, 256), (256, 128), (384, 128))
 
 
 def entries(lst, first, count):
-    return lst[:, first // PER_COL : (first + count) // PER_COL]
+    return lst[:, first // GROUP : (first + count) // GROUP]
 
 
 def tile_picked_pqlayharmprod_none_p_kernel(
@@ -34,52 +38,52 @@ def tile_picked_pqlayharmprod_none_p_kernel(
         keep = ctx.enter_context(tc.tile_pool(name="keep", bufs=1))
         psum = ctx.enter_context(tc.psum_pool(name="psum", bufs=1))
 
-        def list_tile(name, dram):
-            lst = keep.tile([P, S // PER_COL], U16, name=name)
+        def load_list(name, dram):
+            lst = keep.tile([P, S // GROUP], U16, name=name)
             nc.sync.dma_start(lst[:], dram)
             return lst
 
-        one = keep.tile([P, 1], F32, name="one")
-        nc.gpsimd.memset(one[:], 1.0)
-        warm = keep.tile([P, 1], F32, name="warm")
-        nc.scalar.activation(warm[:], one[:], ACT.Abs_reciprocal_sqrt, bias=0.25, scale=0.5)
+        warm_in = keep.tile([P, 1], F32, name="warm_in")
+        nc.gpsimd.memset(warm_in[:], 1.0)
+        warm_out = keep.tile([P, 1], F32, name="warm_out")
+        nc.scalar.activation(warm_out[:], warm_in[:], ACT.Abs_reciprocal_sqrt, bias=0.25, scale=0.5)
 
         d_sc_table = keep.tile([P, G], U8, name="d_sc_table")
-        x_sc_table = keep.tile([P, T], U8, name="x_sc_table", tag="x_sc_table")
+        x_sc_table = keep.tile([P, T], U8, name="x_sc_table")
         nc.vector.memset(d_sc_table[:].bitcast(I32), 0)
         nc.vector.memset(x_sc_table[:].bitcast(I32), 0)
-        k1_list = list_tile("k1_list", k1)
-        offs_list = list_tile("offs_list", offs)
-        n1_list = list_tile("n1_list", n1)
-        n2_list = list_tile("n2_list", n2)
-        n3_list = list_tile("n3_list", n3)
+        k1_list = load_list("k1_list", k1)
+        offs_list = load_list("offs_list", offs)
+        n1_list = load_list("n1_list", n1)
+        n2_list = load_list("n2_list", n2)
+        n3_list = load_list("n3_list", n3)
         d_rows = d_scales[0].bitcast(I32).rearrange("(r e) c -> e r c", e=2)
         for e in range(2):
-            nc.sync.dma_start(d_sc_table[e:P:16, :].bitcast(I32), d_rows[e])
-        d_table = keep.tile([P, G], I32, name="d_table", tag="d_table")
+            nc.sync.dma_start(d_sc_table[e:P:GROUP, :].bitcast(I32), d_rows[e])
+        d_table = keep.tile([P, G], I32, name="d_table")
         nc.sync.dma_start(d_table[:], d_words[0].rearrange("p n t -> p (n t)").bitcast(I32))
         x_rows = x_scales[0].bitcast(I32)
-        for q in range(4):
-            nc.sync.dma_start(x_sc_table[32 * q : 32 * q + 4, :].bitcast(I32), x_rows[4 * q : 4 * q + 4, :])
+        for q in range(P // QUAD):
+            nc.sync.dma_start(x_sc_table[QUAD * q : QUAD * q + 4, :].bitcast(I32), x_rows[4 * q : 4 * q + 4, :])
         x_table = keep.tile([P, T], I32, name="x_table")
         nc.sync.dma_start(x_table[:], x_words[0].rearrange("p n t -> p (n t)").bitcast(I32))
 
-        d_sc_got = keep.tile([P, H], U8, name="d_sc_got")
+        d_sc_got = keep.tile([P, H], U8, name="d_sc_got", tag="d_sc_got")
         nc.vector.tensor_copy(d_sc_got[:], d_sc_table[:].indirect(k1_list[:]))
         d_sc = keep.tile([P, H], U8, name="d_sc", align_bytes=64)
         nc.vector.tensor_copy(
-            d_sc[:].bitcast(I32).rearrange("p (t u) -> p t u", t=PACK),
-            d_sc_got[:].bitcast(I32).rearrange("p (u t) -> p t u", t=PACK),
+            d_sc[:].bitcast(I32).rearrange("p (t u) -> p t u", t=TILES),
+            d_sc_got[:].bitcast(I32).rearrange("p (u t) -> p t u", t=TILES),
         )
         for e in range(2):
-            nc.scalar.dma_start(d_sc[2 + e : P : 32, :].bitcast(I32), d_sc[16 + e : P : 32, :].bitcast(I32))
+            nc.sync.dma_start(d_sc[2 + e : P : QUAD, :].bitcast(I32), d_sc[GROUP + e : P : QUAD, :].bitcast(I32))
 
         d_got = keep.tile([P, H], U32, name="d_got", tag="d_got")
         nc.vector.tensor_copy(d_got[:], d_table[:].bitcast(U32).indirect(k1_list[:]))
         d_codes = keep.tile([P, H], U32, name="d_codes", align_bytes=64)
         nc.vector.tensor_copy(
-            d_codes[:].rearrange("p (t u e) -> p t u e", t=PACK, e=4),
-            d_got[:].rearrange("p (u t e) -> p t u e", t=PACK, e=4),
+            d_codes[:].rearrange("p (t u e) -> p t u e", t=TILES, e=4),
+            d_got[:].rearrange("p (u t e) -> p t u e", t=TILES, e=4),
         )
         x_sc = keep.tile([P, S], U8, name="x_sc", align_bytes=64)
         nc.vector.tensor_copy(x_sc[:], x_sc_table[:].indirect(offs_list[:]))
@@ -88,66 +92,69 @@ def tile_picked_pqlayharmprod_none_p_kernel(
             js = slice(half * HALF, (half + 1) * HALF)
             nc.vector.tensor_copy(x_codes[:, js], x_table[:].bitcast(U32).indirect(entries(offs_list, half * HALF, HALF)))
 
-        w_raw = []
-        w_rows = w1.rearrange("(u t e) m -> t u e m", t=PACK, e=4)
+        w_raw = keep.tile([P, 2, TILES, HALF], F32, name="w_raw", tag="d_sc_got")
+        w_rows = w1.rearrange("(u t e) m -> t u e m", t=TILES, e=4)
         for half in range(2):
-            raw = keep.tile([P, PACK, HALF], F32, name="w_raw%d" % half, tag=("d_table", "x_sc_table")[half])
-            for t in range(PACK):
-                nc.sync.dma_start(raw[:, t, :], w_rows[t][:, :, half * HALF : (half + 1) * HALF])
-            w_raw.append(raw)
-        gain = keep.tile([P, PACK, 8], F32, name="gain", tag="d_got")
-        for t in range(PACK):
-            nc.sync.dma_start(gain[:, t, 0:1], gn.rearrange("(u t e) o -> t u e o", t=PACK, e=4)[t])
+            for t in range(TILES):
+                nc.sync.dma_start(w_raw[:, half, t, :], w_rows[t][:, :, half * HALF : (half + 1) * HALF])
+        gain = keep.tile([P, TILES, 8], F32, name="gain", tag="d_got")
+        for t in range(TILES):
+            nc.sync.dma_start(gain[:, t, 0:1], gn.rearrange("(u t e) o -> t u e o", t=TILES, e=4)[t])
 
-        h = [keep.tile([P, S], F32, name="h%d" % t) for t in range(PACK)]
-        acc = {}
-        for half in range(2):
+        h = [keep.tile([P, S], F32, name="h%d" % t) for t in range(TILES)]
+        parts = [(half, t) for pair in range(2) for half in range(2) for t in (2 * pair, 2 * pair + 1)]
+        h_acc = {}
+        for half, t in parts:
             js = slice(half * HALF, (half + 1) * HALF)
-            for t in range(PACK):
-                cols = slice(t * P, (t + 1) * P)
-                acc[half, t] = psum.tile([P, HALF], F32, name="h_acc%d_%d" % (half, t), tag="bank%d_%d" % (half, t))
-                nc.tensor.matmul_mx(
-                    out=acc[half, t][:], lhsT=d_codes[:, cols].bitcast(FP8X4), lhsT_scale=d_sc[:, cols],
-                    rhs=x_codes[:, js].bitcast(FP8X4), rhs_scale=x_sc[:, js], start=True, stop=True,
-                )
-        for half in range(2):
+            cols = slice(t * P, (t + 1) * P)
+            h_acc[half, t] = psum.tile([P, HALF], F32, name="h_acc%d_%d" % (half, t), tag="bank%d_%d" % (half, t))
+            nc.tensor.matmul_mx(
+                out=h_acc[half, t][:], lhsT=d_codes[:, cols].bitcast(FP8X4), lhsT_scale=d_sc[:, cols],
+                rhs=x_codes[:, js].bitcast(FP8X4), rhs_scale=x_sc[:, js], start=True, stop=True,
+            )
+        for half, t in parts:
             js = slice(half * HALF, (half + 1) * HALF)
-            for t in range(PACK):
-                if half == 1 and t < 2:
-                    nc.vector.tensor_scalar_mul(h[t][:, js], acc[half, t][:], 0.0625)
-                else:
-                    nc.scalar.activation(h[t][:, js], acc[half, t][:], ACT.Copy, scale=0.0625)
-        w_bf = keep.tile([P, PACK * N], BF16, name="w_bf", align_bytes=64)
-        w_view = w_bf[:].rearrange("p (t u e j) -> p u t j e", t=PACK, e=2, j=PACK)
+            if half == 1 and t < 2:
+                nc.vector.tensor_scalar_mul(h[t][:, js], h_acc[half, t][:], H_SCALE)
+            else:
+                nc.scalar.activation(h[t][:, js], h_acc[half, t][:], ACT.Copy, scale=H_SCALE)
+
+        w_bf = keep.tile([P, TILES * N], BF16, name="w_bf", align_bytes=64)
+        w_view = w_bf[:].rearrange("p (t v f a) -> p v t a f", t=TILES, f=2, a=TILES)
+        v_half = HALF // 8
         for half in range(2):
             nc.vector.tensor_copy(
-                w_view[:, 32 * half : 32 * (half + 1)],
-                w_raw[half][:].rearrange("p j (u t e) -> p u t j e", t=PACK, e=2),
+                w_view[:, v_half * half : v_half * (half + 1)],
+                w_raw[:, half].rearrange("p a (v t f) -> p v t a f", t=TILES, f=2),
             )
 
+        h_sq = {}
         nums, invs = [], []
-        for c in range(2):
-            js = slice(c * HALF, (c + 1) * HALF)
-            h_sq = keep.tile([P, PACK, HALF], F32, name="h_sq%d" % c, tag="h_sq%d" % c, align_bytes=64)
-            for t in range(PACK):
-                nc.scalar.activation(h_sq[:, t, :], acc[c, t][:], ACT.Square, scale=0.0625)
-            pa = keep.tile([P, PACK, HALF], F32, name="pa%d" % c)
-            for t in range(PACK):
-                looked_up = h[t][:].indirect(entries(n1_list, c * HALF, HALF))
-                if t < PACK - 1:
+        for c, (first, count) in enumerate(STRETCHES):
+            js = slice(first, first + count)
+            half = first // HALF
+            if half not in h_sq:
+                h_sq[half] = keep.tile([P, TILES, HALF], F32, name="h_sq%d" % half, tag="h_sq%d" % half, align_bytes=64)
+                for t in range(TILES):
+                    nc.scalar.activation(h_sq[half][:, t, :], h_acc[half, t][:], ACT.Square, scale=H_SCALE)
+            pa = keep.tile([P, TILES, count], F32, name="pa%d" % c)
+            for t in range(TILES):
+                looked_up = h[t][:].indirect(entries(n1_list, first, count))
+                if t < TILES - 1:
                     nc.vector.tensor_copy(pa[:, t, :], looked_up)
                 else:
                     nc.scalar.activation(pa[:, t, :], looked_up, ACT.Copy)
-            pa_sq = keep.tile([P, PACK, HALF], F32, name="pa_sq%d" % c, tag="sq_num%d" % c)
+            pa_sq = keep.tile([P, TILES, count], F32, name="pa_sq%d" % c, tag="sq_num%d" % c)
             nc.scalar.activation(pa_sq[:], pa[:], ACT.Square)
-            both = keep.tile([P, PACK, HALF], F32, name="both%d" % c)
-            nc.vector.tensor_tensor(both[:], pa_sq[:], h_sq[:], ALU.add)
-            root = keep.tile([P, PACK, HALF], F32, name="root%d" % c)
+            both = keep.tile([P, TILES, count], F32, name="both%d" % c)
+            in_half = first - half * HALF
+            nc.vector.tensor_tensor(both[:], pa_sq[:], h_sq[half][:, :, in_half : in_half + count], ALU.add)
+            root = keep.tile([P, TILES, count], F32, name="root%d" % c)
             nc.scalar.activation(root[:], both[:], ACT.Abs_reciprocal_sqrt, bias=0.25, scale=0.5)
-            inv = keep.tile([P, PACK, HALF], F32, name="inv%d" % c)
+            inv = keep.tile([P, TILES, count], F32, name="inv%d" % c)
             nc.scalar.activation(inv[:], root[:], ACT.Square)
-            num = keep.tile([P, PACK, HALF], F32, name="num%d" % c, tag="sq_num%d" % c)
-            for t in range(PACK):
+            num = keep.tile([P, TILES, count], F32, name="num%d" % c, tag="sq_num%d" % c)
+            for t in range(TILES):
                 nc.vector.scalar_tensor_tensor(num[:, t, :], h[t][:, js], gain[:, t, 0:1], pa[:, t, :], ALU.mult, ALU.mult)
             nums.append(num)
             invs.append(inv)
@@ -156,50 +163,52 @@ def tile_picked_pqlayharmprod_none_p_kernel(
         w_sc = keep.tile([P, N], U8, name="w_sc", align_bytes=64)
         nc.vector.quantize_mx(out=w_codes[:].bitcast(FP8X4), scales=w_sc[:], in_=w_bf[:])
 
-        h2 = [keep.tile([P, S], F32, name="h2_%d" % t) for t in range(PACK)]
-        acc2 = [psum.tile([P, S], F32, name="h2_acc%d" % t, tag="bank0_%d" % t) for t in range(PACK)]
-        for c in range(2):
-            js = slice(c * HALF, (c + 1) * HALF)
-            z_bf = keep.tile([P, HALF * PACK], BF16, name="z_bf%d" % c, align_bytes=64)
+        h2 = [keep.tile([P, S], F32, name="h2_%d" % t) for t in range(TILES)]
+        h2_acc = [psum.tile([P, S], F32, name="h2_acc%d" % t, tag="bank0_%d" % t) for t in range(TILES)]
+        for c, (first, count) in enumerate(STRETCHES):
+            js = slice(first, first + count)
+            z_bf = keep.tile([P, count * TILES], BF16, name="z_bf%d" % c, align_bytes=64)
             nc.vector.tensor_tensor(
-                z_bf[:].rearrange("p (a i t) -> p a t i", t=PACK, i=2),
-                nums[c][:].rearrange("p t (a i) -> p a t i", i=2),
-                invs[c][:].rearrange("p t (a i) -> p a t i", i=2),
+                z_bf[:].rearrange("p (b n t) -> p b t n", t=TILES, n=2),
+                nums[c][:].rearrange("p t (b n) -> p b t n", n=2),
+                invs[c][:].rearrange("p t (b n) -> p b t n", n=2),
                 ALU.mult,
             )
-            z_codes = keep.tile([P, HALF], U32, name="z_codes%d" % c, align_bytes=64)
-            z_sc = keep.tile([P, HALF], U8, name="z_sc%d" % c, align_bytes=64)
+            z_codes = keep.tile([P, count], U32, name="z_codes%d" % c, align_bytes=64)
+            z_sc = keep.tile([P, count], U8, name="z_sc%d" % c, align_bytes=64)
             nc.vector.quantize_mx(out=z_codes[:].bitcast(FP8X4), scales=z_sc[:], in_=z_bf[:])
-            for t in range(PACK):
+            for t in range(TILES):
                 cols = slice(t * P, (t + 1) * P)
                 nc.tensor.matmul_mx(
-                    out=acc2[t][:, js], lhsT=w_codes[:, cols].bitcast(FP8X4), lhsT_scale=w_sc[:, cols],
+                    out=h2_acc[t][:, js], lhsT=w_codes[:, cols].bitcast(FP8X4), lhsT_scale=w_sc[:, cols],
                     rhs=z_codes[:].bitcast(FP8X4), rhs_scale=z_sc[:], start=True, stop=True,
                 )
-                if c == 1 and t % 2 == 1:
-                    nc.vector.tensor_copy(h2[t][:, js], acc2[t][:, js])
+                if c == len(STRETCHES) - 1 and t % 2 == 1:
+                    nc.vector.tensor_copy(h2[t][:, js], h2_acc[t][:, js])
                 else:
-                    nc.scalar.copy(h2[t][:, js], acc2[t][:, js])
+                    nc.scalar.copy(h2[t][:, js], h2_acc[t][:, js])
 
-        out_rows = out.rearrange("(u t e) j -> t u e j", t=PACK, e=2)
-        for t in range(PACK):
+        out_rows = out.rearrange("(v t f) j -> t v f j", t=TILES, f=2)
+        for t in range(TILES):
+            last_tile = t == TILES - 1
+            pieces = LAST_TILE_PIECES if last_tile else ((0, HALF), (HALF, HALF))
             res = keep.tile([P, S], F32, name="res%d" % t)
-            for half in range(2):
-                js = slice(half * HALF, (half + 1) * HALF)
-                left = keep.tile([P, HALF], F32, name="left%d_%d" % (t, half))
-                looked_up = h2[t][:].indirect(entries(n2_list, half * HALF, HALF))
-                if t == 0 and half == 0:
-                    nc.vector.tensor_copy(left[:], looked_up)
+            for first, count in pieces:
+                js = slice(first, first + count)
+                left = keep.tile([P, count], F32, name="left%d_%d" % (t, first))
+                by_n2 = h2[t][:].indirect(entries(n2_list, first, count))
+                by_n3 = h2[t][:].indirect(entries(n3_list, first, count))
+                if t == 0 and first == 0:
+                    nc.vector.tensor_copy(left[:], by_n2)
                 else:
-                    nc.scalar.activation(left[:], looked_up, ACT.Copy)
-                looked_up = h2[t][:].indirect(entries(n3_list, half * HALF, HALF))
-                if t < PACK - 1 or half == 0:
-                    nc.vector.tensor_tensor(res[:, js], looked_up, left[:], ALU.mult)
-                else:
-                    right = keep.tile([P, HALF], F32, name="right%d" % half)
-                    nc.scalar.activation(right[:], looked_up, ACT.Copy)
+                    nc.scalar.activation(left[:], by_n2, ACT.Copy)
+                if last_tile and first + count == S:
+                    right = keep.tile([P, count], F32, name="right")
+                    nc.scalar.activation(right[:], by_n3, ACT.Copy)
                     nc.vector.tensor_tensor(res[:, js], right[:], left[:], ALU.mult)
-                if t == PACK - 1:
+                else:
+                    nc.vector.tensor_tensor(res[:, js], by_n3, left[:], ALU.mult)
+                if last_tile:
                     nc.sync.dma_start(out_rows[t][:, :, js], res[:, js])
-            if t < PACK - 1:
+            if not last_tile:
                 nc.sync.dma_start(out_rows[t], res[:])

@@ -1,6 +1,7 @@
 from contextlib import ExitStack
 
 import concourse.mybir as mybir
+from concourse.masks import make_identity
 
 K, T, S, N, G, H = 512, 2048, 512, 512, 2048, 512
 FLOPS = 2 * K * H * S + 2 * H * N * S
@@ -22,7 +23,7 @@ QUAD = 32
 HALF = 256
 H_SCALE = 0.0625
 
-STRETCHES = ((0, 256), (256, 128), (384, 128))
+QUARTERS = 4
 LAST_TILE_PIECES = ((0, 256), (256, 128), (384, 128))
 
 
@@ -128,65 +129,80 @@ def tile_picked_pqlayharmprod_none_p_kernel(
                 w_raw[:, half].rearrange("p a (v t f) -> p v t a f", t=TILES, f=2),
             )
 
-        h_sq = {}
+        ident = keep.tile([P, P], F32, name="ident")
+        make_identity(nc, ident[:])
         nums, invs = [], []
-        for c, (first, count) in enumerate(STRETCHES):
-            js = slice(first, first + count)
-            half = first // HALF
-            if half not in h_sq:
-                h_sq[half] = keep.tile([P, TILES, HALF], F32, name="h_sq%d" % half, tag="h_sq%d" % half, align_bytes=64)
-                for t in range(TILES):
-                    nc.scalar.activation(h_sq[half][:, t, :], h_acc[half, t][:], ACT.Square, scale=H_SCALE)
-            pa = keep.tile([P, TILES, count], F32, name="pa%d" % c)
+        for half in range(2):
+            js = slice(half * HALF, (half + 1) * HALF)
+            h_sq = keep.tile([P, TILES, HALF], F32, name="h_sq%d" % half)
             for t in range(TILES):
-                looked_up = h[t][:].indirect(entries(n1_list, first, count))
-                if t < TILES - 1:
+                nc.scalar.activation(h_sq[:, t, :], h_acc[half, t][:], ACT.Square, scale=H_SCALE)
+            pa = keep.tile([P, TILES, HALF], F32, name="pa%d" % half)
+            for t in range(TILES):
+                looked_up = h[t][:].indirect(entries(n1_list, half * HALF, HALF))
+                if t < TILES - 1 or half == 1:
                     nc.vector.tensor_copy(pa[:, t, :], looked_up)
                 else:
                     nc.scalar.activation(pa[:, t, :], looked_up, ACT.Copy)
-            pa_sq = keep.tile([P, TILES, count], F32, name="pa_sq%d" % c, tag="sq_num%d" % c)
-            nc.scalar.activation(pa_sq[:], pa[:], ACT.Square)
-            both = keep.tile([P, TILES, count], F32, name="both%d" % c)
-            in_half = first - half * HALF
-            nc.vector.tensor_tensor(both[:], pa_sq[:], h_sq[half][:, :, in_half : in_half + count], ALU.add)
-            root = keep.tile([P, TILES, count], F32, name="root%d" % c)
-            nc.scalar.activation(root[:], both[:], ACT.Abs_reciprocal_sqrt, bias=0.25, scale=0.5)
-            inv = keep.tile([P, TILES, count], F32, name="inv%d" % c)
-            nc.scalar.activation(inv[:], root[:], ACT.Square)
-            num = keep.tile([P, TILES, count], F32, name="num%d" % c, tag="sq_num%d" % c)
+            pa_sq = keep.tile([P, TILES, HALF], F32, name="pa_sq%d" % half, tag="sq_num%d" % half)
+            for k in range(2):
+                ks = slice(k * P, (k + 1) * P)
+                nc.scalar.activation(pa_sq[:, :, ks], pa[:, :, ks], ACT.Square)
+            for k in range(2):
+                ks = slice(k * P, (k + 1) * P)
+                both = psum.tile([P, TILES, P], F32, name="both%d_%d" % (half, k), tag="bank%d_%d" % (half, k))
+                for t in range(TILES):
+                    nc.tensor.matmul(both[:, t, :], h_sq[:, t, ks], ident[:], start=True, stop=False, is_transpose=True)
+                    nc.tensor.matmul(both[:, t, :], pa_sq[:, t, ks], ident[:], start=False, stop=True, is_transpose=True)
+                root = keep.tile([P, TILES, P], F32, name="root%d_%d" % (half, k))
+                nc.scalar.activation(root[:], both[:], ACT.Abs_reciprocal_sqrt, bias=0.25, scale=0.5)
+                inv_turned = keep.tile([P, TILES, P], F32, name="inv_turned%d_%d" % (half, k))
+                nc.scalar.activation(inv_turned[:], root[:], ACT.Square)
+                inv = psum.tile([P, TILES, P], F32, name="inv%d_%d" % (half, k), tag="bank%d_%d" % (half, 2 + k))
+                for t in range(TILES):
+                    nc.tensor.transpose(inv[:, t, :], inv_turned[:, t, :], ident[:])
+                invs.append(inv)
+            num = keep.tile([P, TILES, HALF], F32, name="num%d" % half, tag="sq_num%d" % half)
             for t in range(TILES):
                 nc.vector.scalar_tensor_tensor(num[:, t, :], h[t][:, js], gain[:, t, 0:1], pa[:, t, :], ALU.mult, ALU.mult)
             nums.append(num)
-            invs.append(inv)
 
-        w_codes = keep.tile([P, N], U32, name="w_codes", tag="h_sq0", align_bytes=64)
+        w_codes = keep.tile([P, N], U32, name="w_codes", align_bytes=64)
         w_sc = keep.tile([P, N], U8, name="w_sc", align_bytes=64)
         nc.vector.quantize_mx(out=w_codes[:].bitcast(FP8X4), scales=w_sc[:], in_=w_bf[:])
 
         h2 = [keep.tile([P, S], F32, name="h2_%d" % t) for t in range(TILES)]
-        h2_acc = [psum.tile([P, S], F32, name="h2_acc%d" % t, tag="bank0_%d" % t) for t in range(TILES)]
-        for c, (first, count) in enumerate(STRETCHES):
-            js = slice(first, first + count)
-            z_bf = keep.tile([P, count * TILES], BF16, name="z_bf%d" % c, align_bytes=64)
+        for c in range(QUARTERS):
+            last_quarter = c == QUARTERS - 1
+            js = slice(c * P, (c + 1) * P)
+            ks = slice((c % 2) * P, (c % 2 + 1) * P)
+            z_bf = keep.tile([P, P * TILES], BF16, name="z_bf%d" % c, align_bytes=64)
             nc.vector.tensor_tensor(
                 z_bf[:].rearrange("p (b n t) -> p b t n", t=TILES, n=2),
-                nums[c][:].rearrange("p t (b n) -> p b t n", n=2),
+                nums[c // 2][:, :, ks].rearrange("p t (b n) -> p b t n", n=2),
                 invs[c][:].rearrange("p t (b n) -> p b t n", n=2),
                 ALU.mult,
             )
-            z_codes = keep.tile([P, count], U32, name="z_codes%d" % c, align_bytes=64)
-            z_sc = keep.tile([P, count], U8, name="z_sc%d" % c, align_bytes=64)
+            z_codes = keep.tile([P, P], U32, name="z_codes%d" % c, align_bytes=64)
+            z_sc = keep.tile([P, P], U8, name="z_sc%d" % c, align_bytes=64)
             nc.vector.quantize_mx(out=z_codes[:].bitcast(FP8X4), scales=z_sc[:], in_=z_bf[:])
+            if last_quarter:
+                free_banks = ("bank0_3", "bank1_0", "bank1_1", "bank0_0")
+                accs = [psum.tile([P, P], F32, name="h2_last%d" % t, tag=free_banks[t])[:] for t in range(TILES)]
+            else:
+                shared = psum.tile([P, TILES, P], F32, name="h2_acc%d" % c, tag="bank0_%d" % c)
+                accs = [shared[:, t, :] for t in range(TILES)]
             for t in range(TILES):
                 cols = slice(t * P, (t + 1) * P)
                 nc.tensor.matmul_mx(
-                    out=h2_acc[t][:, js], lhsT=w_codes[:, cols].bitcast(FP8X4), lhsT_scale=w_sc[:, cols],
+                    out=accs[t], lhsT=w_codes[:, cols].bitcast(FP8X4), lhsT_scale=w_sc[:, cols],
                     rhs=z_codes[:].bitcast(FP8X4), rhs_scale=z_sc[:], start=True, stop=True,
                 )
-                if c == len(STRETCHES) - 1 and t % 2 == 1:
-                    nc.vector.tensor_copy(h2[t][:, js], h2_acc[t][:, js])
+            for t in range(TILES):
+                if last_quarter and t % 2 == 1:
+                    nc.vector.tensor_copy(h2[t][:, js], accs[t])
                 else:
-                    nc.scalar.copy(h2[t][:, js], h2_acc[t][:, js])
+                    nc.scalar.copy(h2[t][:, js], accs[t])
 
         out_rows = out.rearrange("(v t f) j -> t v f j", t=TILES, f=2)
         for t in range(TILES):

from contextlib import ExitStack

import concourse.mybir as mybir
from concourse.masks import make_identity

K, T, S, N, G, H = 512, 2048, 512, 512, 2048, 512
FLOPS = 2 * K * H * S + 2 * H * N * S

F32 = mybir.dt.float32
BF16 = mybir.dt.bfloat16
I32 = mybir.dt.int32
U32 = mybir.dt.uint32
U16 = mybir.dt.uint16
U8 = mybir.dt.uint8
FP8X4 = mybir.dt.float8_e4m3fn_x4
ACT = mybir.ActivationFunctionType
ALU = mybir.AluOpType

P = 128
TILES = 4
GROUP = 16
QUAD = 32
HALF = 256
H_SCALE = 0.0625

QUARTERS = 4
LAST_TILE_PIECES = ((0, 256), (256, 128), (384, 128))


def entries(lst, first, count):
    return lst[:, first // GROUP : (first + count) // GROUP]


def tile_picked_pqlayharmprod_none_p_kernel(
    tc, x_words, x_scales, d_words, d_scales, gn, w1, offs, k1, n1, n2, n3, out
):
    nc = tc.nc
    with ExitStack() as ctx:
        keep = ctx.enter_context(tc.tile_pool(name="keep", bufs=1))
        psum = ctx.enter_context(tc.psum_pool(name="psum", bufs=1))

        def load_list(name, dram):
            lst = keep.tile([P, S // GROUP], U16, name=name)
            nc.sync.dma_start(lst[:], dram)
            return lst

        warm_in = keep.tile([P, 1], F32, name="warm_in")
        nc.gpsimd.memset(warm_in[:], 1.0)
        warm_out = keep.tile([P, 1], F32, name="warm_out")
        nc.scalar.activation(warm_out[:], warm_in[:], ACT.Abs_reciprocal_sqrt, bias=0.25, scale=0.5)

        d_sc_table = keep.tile([P, G], U8, name="d_sc_table")
        x_sc_table = keep.tile([P, T], U8, name="x_sc_table")
        nc.vector.memset(d_sc_table[:].bitcast(I32), 0)
        nc.vector.memset(x_sc_table[:].bitcast(I32), 0)
        k1_list = load_list("k1_list", k1)
        offs_list = load_list("offs_list", offs)
        n1_list = load_list("n1_list", n1)
        n2_list = load_list("n2_list", n2)
        n3_list = load_list("n3_list", n3)
        d_rows = d_scales[0].bitcast(I32).rearrange("(r e) c -> e r c", e=2)
        for e in range(2):
            nc.sync.dma_start(d_sc_table[e:P:GROUP, :].bitcast(I32), d_rows[e])
        d_table = keep.tile([P, G], I32, name="d_table")
        nc.sync.dma_start(d_table[:], d_words[0].rearrange("p n t -> p (n t)").bitcast(I32))
        x_rows = x_scales[0].bitcast(I32)
        for q in range(P // QUAD):
            nc.sync.dma_start(x_sc_table[QUAD * q : QUAD * q + 4, :].bitcast(I32), x_rows[4 * q : 4 * q + 4, :])
        x_table = keep.tile([P, T], I32, name="x_table")
        nc.sync.dma_start(x_table[:], x_words[0].rearrange("p n t -> p (n t)").bitcast(I32))

        d_sc_got = keep.tile([P, H], U8, name="d_sc_got", tag="d_sc_got")
        nc.vector.tensor_copy(d_sc_got[:], d_sc_table[:].indirect(k1_list[:]))
        d_sc = keep.tile([P, H], U8, name="d_sc", align_bytes=64)
        nc.vector.tensor_copy(
            d_sc[:].bitcast(I32).rearrange("p (t u) -> p t u", t=TILES),
            d_sc_got[:].bitcast(I32).rearrange("p (u t) -> p t u", t=TILES),
        )
        for e in range(2):
            nc.sync.dma_start(d_sc[2 + e : P : QUAD, :].bitcast(I32), d_sc[GROUP + e : P : QUAD, :].bitcast(I32))

        d_got = keep.tile([P, H], U32, name="d_got", tag="d_got")
        nc.vector.tensor_copy(d_got[:], d_table[:].bitcast(U32).indirect(k1_list[:]))
        d_codes = keep.tile([P, H], U32, name="d_codes", align_bytes=64)
        nc.vector.tensor_copy(
            d_codes[:].rearrange("p (t u e) -> p t u e", t=TILES, e=4),
            d_got[:].rearrange("p (u t e) -> p t u e", t=TILES, e=4),
        )
        x_sc = keep.tile([P, S], U8, name="x_sc", align_bytes=64)
        nc.vector.tensor_copy(x_sc[:], x_sc_table[:].indirect(offs_list[:]))
        x_codes = keep.tile([P, S], U32, name="x_codes", align_bytes=64)
        for half in range(2):
            js = slice(half * HALF, (half + 1) * HALF)
            nc.vector.tensor_copy(x_codes[:, js], x_table[:].bitcast(U32).indirect(entries(offs_list, half * HALF, HALF)))

        w_raw = keep.tile([P, 2, TILES, HALF], F32, name="w_raw", tag="d_sc_got")
        w_rows = w1.rearrange("(u t e) m -> t u e m", t=TILES, e=4)
        for half in range(2):
            for t in range(TILES):
                nc.sync.dma_start(w_raw[:, half, t, :], w_rows[t][:, :, half * HALF : (half + 1) * HALF])
        gain = keep.tile([P, TILES, 8], F32, name="gain", tag="d_got")
        for t in range(TILES):
            nc.sync.dma_start(gain[:, t, 0:1], gn.rearrange("(u t e) o -> t u e o", t=TILES, e=4)[t])

        h = [keep.tile([P, S], F32, name="h%d" % t) for t in range(TILES)]
        parts = [(half, t) for pair in range(2) for half in range(2) for t in (2 * pair, 2 * pair + 1)]
        h_acc = {}
        for half, t in parts:
            js = slice(half * HALF, (half + 1) * HALF)
            cols = slice(t * P, (t + 1) * P)
            h_acc[half, t] = psum.tile([P, HALF], F32, name="h_acc%d_%d" % (half, t), tag="bank%d_%d" % (half, t))
            nc.tensor.matmul_mx(
                out=h_acc[half, t][:], lhsT=d_codes[:, cols].bitcast(FP8X4), lhsT_scale=d_sc[:, cols],
                rhs=x_codes[:, js].bitcast(FP8X4), rhs_scale=x_sc[:, js], start=True, stop=True,
            )
        for half, t in parts:
            js = slice(half * HALF, (half + 1) * HALF)
            if half == 1 and t < 2:
                nc.vector.tensor_scalar_mul(h[t][:, js], h_acc[half, t][:], H_SCALE)
            else:
                nc.scalar.activation(h[t][:, js], h_acc[half, t][:], ACT.Copy, scale=H_SCALE)

        w_bf = keep.tile([P, TILES * N], BF16, name="w_bf", align_bytes=64)
        w_view = w_bf[:].rearrange("p (t v f a) -> p v t a f", t=TILES, f=2, a=TILES)
        v_half = HALF // 8
        for half in range(2):
            nc.vector.tensor_copy(
                w_view[:, v_half * half : v_half * (half + 1)],
                w_raw[:, half].rearrange("p a (v t f) -> p v t a f", t=TILES, f=2),
            )

        ident = keep.tile([P, P], F32, name="ident")
        make_identity(nc, ident[:])
        nums, invs = [], []
        for half in range(2):
            js = slice(half * HALF, (half + 1) * HALF)
            h_sq = keep.tile([P, TILES, HALF], F32, name="h_sq%d" % half)
            for t in range(TILES):
                nc.scalar.activation(h_sq[:, t, :], h_acc[half, t][:], ACT.Square, scale=H_SCALE)
            pa = keep.tile([P, TILES, HALF], F32, name="pa%d" % half)
            for t in range(TILES):
                looked_up = h[t][:].indirect(entries(n1_list, half * HALF, HALF))
                if t < TILES - 1 or half == 1:
                    nc.vector.tensor_copy(pa[:, t, :], looked_up)
                else:
                    nc.scalar.activation(pa[:, t, :], looked_up, ACT.Copy)
            pa_sq = keep.tile([P, TILES, HALF], F32, name="pa_sq%d" % half, tag="sq_num%d" % half)
            for k in range(2):
                ks = slice(k * P, (k + 1) * P)
                nc.scalar.activation(pa_sq[:, :, ks], pa[:, :, ks], ACT.Square)
            for k in range(2):
                ks = slice(k * P, (k + 1) * P)
                both = psum.tile([P, TILES, P], F32, name="both%d_%d" % (half, k), tag="bank%d_%d" % (half, k))
                for t in range(TILES):
                    nc.tensor.matmul(both[:, t, :], h_sq[:, t, ks], ident[:], start=True, stop=False, is_transpose=True)
                    nc.tensor.matmul(both[:, t, :], pa_sq[:, t, ks], ident[:], start=False, stop=True, is_transpose=True)
                root = keep.tile([P, TILES, P], F32, name="root%d_%d" % (half, k))
                nc.scalar.activation(root[:], both[:], ACT.Abs_reciprocal_sqrt, bias=0.25, scale=0.5)
                inv_turned = keep.tile([P, TILES, P], F32, name="inv_turned%d_%d" % (half, k))
                nc.scalar.activation(inv_turned[:], root[:], ACT.Square)
                inv = psum.tile([P, TILES, P], F32, name="inv%d_%d" % (half, k), tag="bank%d_%d" % (half, 2 + k))
                for t in range(TILES):
                    nc.tensor.transpose(inv[:, t, :], inv_turned[:, t, :], ident[:])
                invs.append(inv)
            num = keep.tile([P, TILES, HALF], F32, name="num%d" % half, tag="sq_num%d" % half)
            for t in range(TILES):
                nc.vector.scalar_tensor_tensor(num[:, t, :], h[t][:, js], gain[:, t, 0:1], pa[:, t, :], ALU.mult, ALU.mult)
            nums.append(num)

        w_codes = keep.tile([P, N], U32, name="w_codes", align_bytes=64)
        w_sc = keep.tile([P, N], U8, name="w_sc", align_bytes=64)
        nc.vector.quantize_mx(out=w_codes[:].bitcast(FP8X4), scales=w_sc[:], in_=w_bf[:])

        h2 = [keep.tile([P, S], F32, name="h2_%d" % t) for t in range(TILES)]
        for c in range(QUARTERS):
            last_quarter = c == QUARTERS - 1
            js = slice(c * P, (c + 1) * P)
            ks = slice((c % 2) * P, (c % 2 + 1) * P)
            z_bf = keep.tile([P, P * TILES], BF16, name="z_bf%d" % c, align_bytes=64)
            nc.vector.tensor_tensor(
                z_bf[:].rearrange("p (b n t) -> p b t n", t=TILES, n=2),
                nums[c // 2][:, :, ks].rearrange("p t (b n) -> p b t n", n=2),
                invs[c][:].rearrange("p t (b n) -> p b t n", n=2),
                ALU.mult,
            )
            z_codes = keep.tile([P, P], U32, name="z_codes%d" % c, align_bytes=64)
            z_sc = keep.tile([P, P], U8, name="z_sc%d" % c, align_bytes=64)
            nc.vector.quantize_mx(out=z_codes[:].bitcast(FP8X4), scales=z_sc[:], in_=z_bf[:])
            if last_quarter:
                free_banks = ("bank0_3", "bank1_0", "bank1_1", "bank0_0")
                accs = [psum.tile([P, P], F32, name="h2_last%d" % t, tag=free_banks[t])[:] for t in range(TILES)]
            else:
                shared = psum.tile([P, TILES, P], F32, name="h2_acc%d" % c, tag="bank0_%d" % c)
                accs = [shared[:, t, :] for t in range(TILES)]
            for t in range(TILES):
                cols = slice(t * P, (t + 1) * P)
                nc.tensor.matmul_mx(
                    out=accs[t], lhsT=w_codes[:, cols].bitcast(FP8X4), lhsT_scale=w_sc[:, cols],
                    rhs=z_codes[:].bitcast(FP8X4), rhs_scale=z_sc[:], start=True, stop=True,
                )
            for t in range(TILES):
                if last_quarter and t % 2 == 1:
                    nc.vector.tensor_copy(h2[t][:, js], accs[t])
                else:
                    nc.scalar.copy(h2[t][:, js], accs[t])

        out_rows = out.rearrange("(v t f) j -> t v f j", t=TILES, f=2)
        for t in range(TILES):
            last_tile = t == TILES - 1
            pieces = LAST_TILE_PIECES if last_tile else ((0, HALF), (HALF, HALF))
            res = keep.tile([P, S], F32, name="res%d" % t)
            for first, count in pieces:
                js = slice(first, first + count)
                left = keep.tile([P, count], F32, name="left%d_%d" % (t, first))
                by_n2 = h2[t][:].indirect(entries(n2_list, first, count))
                by_n3 = h2[t][:].indirect(entries(n3_list, first, count))
                if t == 0 and first == 0:
                    nc.vector.tensor_copy(left[:], by_n2)
                else:
                    nc.scalar.activation(left[:], by_n2, ACT.Copy)
                if last_tile and first + count == S:
                    right = keep.tile([P, count], F32, name="right")
                    nc.scalar.activation(right[:], by_n3, ACT.Copy)
                    nc.vector.tensor_tensor(res[:, js], right[:], left[:], ALU.mult)
                else:
                    nc.vector.tensor_tensor(res[:, js], by_n3, left[:], ALU.mult)
                if last_tile:
                    nc.sync.dma_start(out_rows[t][:, :, js], res[:, js])
            if not last_tile:
                nc.sync.dma_start(out_rows[t], res[:])
